import numpy as np, ml_dtypes
CORES = [4,12,20,28,44,60,76,84,92,108,116,124]
N = 12
import mx_ref
NC, G, D = 512, 2, 64
C = np.float32(0.029)
BF = ml_dtypes.bfloat16
def cut(t, i, w=512):
    return t[:, w * i:w * i + w]
def tile(rs):
    return np.stack(rs, axis=2).reshape(128, -1).astype(BF)
def act(Z):
    return [np.maximum(s * z, 0) * C for z in Z for s in (1, -1)]
def taps(w, i, e):
    return mx_ref.matmul(mx_ref.quantize(cut(w, 2 * i)), mx_ref.quantize(e[:, :4 * NC])) + mx_ref.matmul(mx_ref.quantize(cut(w, 2 * i + 1)), mx_ref.quantize(e[:, 4 * D:4 * D + 4 * NC]))
def setup_inputs(rng):
    def f(*shape):
        return mx_ref.flush((rng.standard_normal(shape, dtype=np.float32) * np.exp2(rng.integers(-2, 3, shape[:-1] + (1,)))).astype(BF))
    return {"x": f(N, 128, 4 * NC), "wa": np.broadcast_to(f(1, 128, 2 * G * 512), (N, 128, 2 * G * 512)).copy(), "wb": f(N, 128, 2 * 512)}
def setup_inputs_blocks(rng):
    d = setup_inputs(rng)
    for k in ("x", "wb"): d[k] = mx_ref.spread(d[k], rng, 2)
    return d
def setup_inputs_wide(rng):
    d = setup_inputs(rng)
    for k in ("wb",): d[k] = mx_ref.flush((d[k].astype(np.float32) * np.exp2(rng.integers(-6, 7, (N, 1, 1))).astype(np.float32)).astype(BF))
    return d
def setup_inputs_zeros(rng):
    d = setup_inputs(rng); v = d["x"].reshape(N, 128, -1, 4).copy()
    v[np.broadcast_to((rng.random((N, 1, v.shape[2], 1)) < 0.33), v.shape)] = 0
    d["x"] = v.reshape(d["x"].shape)
    return d
def reference(x, wa, wb):
    edge = lambda t, r: np.concatenate([t[(r - 1) % N][:, 4 * (NC - D):], t[r]], axis=1)
    u = [tile(act([taps(wa[r], i, edge(x, r)) for i in range(G)])) for r in range(N)]
    y = np.zeros((N, 128, NC), np.float32)
    for r in range(N):
        y[r] = taps(wb[r], 0, edge(u, r))
    return {"y": y}

from concourse.mybir import dt, AluOpType, ActivationFunctionType

NC, D = 512, 64
H = 2 * D
C = 0.029

SCRATCH = {
    "xb": ("sbuf", [128, 4 * NC], "bfloat16"),
    "wab": ("sbuf", [128, 4 * NC], "bfloat16"),
    "wbb": ("sbuf", [128, 2 * NC], "bfloat16"),
    "ub": ("sbuf", [128, 4 * (NC + D)], "bfloat16"),
    "yb": ("sbuf", [128, NC], "float32"),
    "xq": ("sbuf", [128, NC + H], "float8_e4m3fn_x4"),
    "xs": ("sbuf", [128, NC + H], "uint8"),
    "waq": ("sbuf", [128, NC], "float8_e4m3fn_x4"),
    "was": ("sbuf", [128, NC], "uint8"),
    "wbq": ("sbuf", [128, 256], "float8_e4m3fn_x4"),
    "wbs": ("sbuf", [128, 256], "uint8"),
    "uq": ("sbuf", [128, NC + D], "float8_e4m3fn_x4"),
    "us": ("sbuf", [128, NC + D], "uint8"),
    "pm0": ("psum", [128, 512], "float32"),
    "pm1": ("psum", [128, 512], "float32"),
    "ph0": ("psum", [128, 512], "float32"),
    "ph1": ("psum", [128, 512], "float32"),
    "pya": ("psum", [128, 512], "float32"),
    "pyb": ("psum", [128, 512], "float32"),
}
SEMAPHORES = ["l_xh", "l_xm", "l_wa", "l_wb",
              "q_xh", "q_xm", "q_wa", "q_wb", "q_um", "q_uh",
              "z_m0", "z_m1", "z_h0", "z_h1", "z_ya", "z_yb",
              "u_m", "u_h", "c_ya", "c_yb", "st_a", "st_b",
              "h_c", "h_s",
              "s_c", "s_s"]

ENGINES = 8


def engines(topo, src, dst, n):
    m, out, k = topo.mask(src, dst), 0, 0
    for b in range(16):
        if m >> b & 1 and k < n:
            out |= 1 << b
            k += 1
    return out, k


def relays(T, topo, src, dst):
    near = [c for c in range(8 * len(range(16)))
            if topo.chip(c) == topo.chip(src) and c != src and T.rank_of(c) is None and topo.may_write(c, dst)]
    near.sort(key=lambda c: (topo.die(c) != topo.die(src), c))
    return near[0], near[1]


def send(g, T, topo, core, dst, codes, lo):
    rid, pid, _ = topo.addr(dst)
    m, k = engines(topo, core, dst, ENGINES)
    if codes:
        g.remote_dma(T.xq[:, 0:H].bitcast(dt.uint8), T.xq[:, lo:lo + H].bitcast(dt.uint8), T.sem.h_c, T.sem.s_c, pid, rid, m)
    else:
        g.remote_dma(T.xs[:, 0:H], T.xs[:, lo:lo + H], T.sem.h_s, T.sem.s_s, pid, rid, m)
    return k


def rank_program(g, core, T, topo):
    cores = T.cores
    n = len(cores)
    rank = T.rank_of(core)
    S = T.sem

    if rank is None:
        for r in range(n):
            src, dst = cores[r], cores[(r + 1) % n]
            if topo.chip(src) != topo.chip(core) or topo.may_write(src, dst):
                continue
            a, b = relays(T, topo, src, dst)
            if core == a:
                g.wait_ge(S.h_c, engines(topo, src, a, ENGINES)[1])
                k = send(g, T, topo, core, dst, True, 0)
                g.wait_ge(S.s_c, k)
            elif core == b:
                g.wait_ge(S.h_s, engines(topo, src, b, ENGINES)[1])
                k = send(g, T, topo, core, dst, False, 0)
                g.wait_ge(S.s_s, k)
        return

    nxt = cores[(rank + 1) % n]
    prv = cores[(rank - 1) % n]
    to_c, to_s = (nxt, nxt) if topo.may_write(core, nxt) else relays(T, topo, core, nxt)
    from_c, from_s = (prv, prv) if topo.may_write(prv, core) else relays(T, topo, prv, core)
    g.wait_ge(S.q_xh, 1)
    kc = send(g, T, topo, core, to_c, True, NC)
    ks = send(g, T, topo, core, to_s, False, NC)
    g.wait_ge(S.s_s, ks)

    X0 = 4 * (NC - H)
    sy, ac, ve, te = g.sync, g.scalar, g.vector, g.tensor
    sy.dma_start(T.xb[0:64, X0:4 * NC], T.x[0:64, X0:4 * NC]).then_inc(S.l_xh, 16)
    ac.dma_start(T.xb[64:128, X0:4 * NC], T.x[64:128, X0:4 * NC]).then_inc(S.l_xh, 16)
    sy.dma_start(T.wab[:], T.wa[:]).then_inc(S.l_wa, 16)
    ac.dma_start(T.xb[:, 0:X0], T.x[:, 0:X0]).then_inc(S.l_xm, 16)
    sy.wait_ge(S.s_c, kc)
    sy.dma_start(T.wbb[:], T.wb[:]).then_inc(S.l_wb, 16)
    sy.wait_ge(S.c_yb, 1)
    sy.dma_start(T.y[:, H:NC], T.yb[:, H:NC]).then_inc(S.st_b, 16)
    sy.wait_ge(S.c_ya, 1)
    sy.dma_start(T.y[:, 0:H], T.yb[:, 0:H]).then_inc(S.st_a, 16)
    sy.wait_ge(S.st_b, 16)
    sy.wait_ge(S.st_a, 16)

    def layer1(out, i, c0, w):
        for t in (0, 1):
            k = 128 * (2 * i + t)
            a = c0 + t * D
            p = te.matmul_mx(out[:, 0:w], T.waq[:, k:k + 128], T.was[:, k:k + 128],
                             T.xq[:, a:a + w], T.xs[:, a:a + w], t == 0, t == 1)
        return p

    def layer2(out, c0, w):
        for t in (0, 1):
            a = c0 + t * D
            p = te.matmul_mx(out[:, 0:w], T.wbq[:, 128 * t:128 * t + 128], T.wbs[:, 128 * t:128 * t + 128],
                             T.uq[:, a:a + w], T.us[:, a:a + w], t == 0, t == 1)
        return p

    M = NC + D - H
    te.wait_ge(S.q_xh, 1)
    te.wait_ge(S.q_xm, 1)
    te.wait_ge(S.q_wa, 1)
    layer1(T.pm0, 0, H, M).then_inc(S.z_m0, 1)
    layer1(T.pm1, 1, H, M).then_inc(S.z_m1, 1)
    te.wait_ge(S.q_um, 1)
    te.wait_ge(S.q_wb, 1)
    layer2(T.pyb, H, NC - H).then_inc(S.z_yb, 1)
    te.wait_ge(S.h_c, engines(topo, from_c, core, ENGINES)[1])
    te.wait_ge(S.h_s, engines(topo, from_s, core, ENGINES)[1])
    layer1(T.ph0, 0, 0, H).then_inc(S.z_h0, 1)
    layer1(T.ph1, 1, 0, H).then_inc(S.z_h1, 1)
    te.wait_ge(S.q_uh, 1)
    layer2(T.pya, 0, H).then_inc(S.z_ya, 1)

    def act_scalar(z, c0, w, sem):
        for b, s in ((0, C), (1, -C)):
            ac.activation(T.ub[:, 4 * c0 + b:4 * (c0 + w):4], z[:, 0:w], ActivationFunctionType.Relu, scale=s).then_inc(sem, 1)

    def act_vector(z, c0, w, sem):
        for b, s in ((2, C), (3, -C)):
            ve.tensor_scalar(T.ub[:, 4 * c0 + b:4 * (c0 + w):4], z[:, 0:w], s, 0.0, AluOpType.mult, AluOpType.max).then_inc(sem, 1)

    ac.wait_ge(S.z_m0, 1)
    act_scalar(T.pm0, H, M, S.u_m)
    ac.wait_ge(S.z_yb, 1)
    ac.activation(T.yb[:, H:NC], T.pyb[:, 0:NC - H], ActivationFunctionType.Copy).then_inc(S.c_yb, 1)
    ac.wait_ge(S.z_h0, 1)
    act_scalar(T.ph0, 0, H, S.u_h)

    ve.wait_ge(S.l_xh, 32)
    ve.quantize_mx(T.xq[:, NC:NC + H], T.xs[:, NC:NC + H], T.xb[:, X0:4 * NC]).then_inc(S.q_xh, 1)
    ve.wait_ge(S.l_xm, 16)
    ve.quantize_mx(T.xq[:, H:NC], T.xs[:, H:NC], T.xb[:, 0:X0]).then_inc(S.q_xm, 1)
    ve.wait_ge(S.l_wa, 16)
    ve.quantize_mx(T.waq[:], T.was[:], T.wab[:]).then_inc(S.q_wa, 1)
    ve.wait_ge(S.z_m1, 1)
    act_vector(T.pm1, H, M, S.u_m)
    ve.wait_ge(S.u_m, 4)
    ve.quantize_mx(T.uq[:, H:H + M], T.us[:, H:H + M], T.ub[:, 4 * H:4 * (H + M)]).then_inc(S.q_um, 1)
    ve.wait_ge(S.l_wb, 16)
    ve.quantize_mx(T.wbq[:], T.wbs[:], T.wbb[:]).then_inc(S.q_wb, 1)
    ve.wait_ge(S.z_h1, 1)
    act_vector(T.ph1, 0, H, S.u_h)
    ve.wait_ge(S.u_h, 4)
    ve.quantize_mx(T.uq[:, 0:H], T.us[:, 0:H], T.ub[:, 0:4 * H]).then_inc(S.q_uh, 1)
    ve.wait_ge(S.z_ya, 1)
    ve.tensor_copy(T.yb[:, 0:H], T.pya[:, 0:H]).then_inc(S.c_ya, 1)
